import numpy as np
import ml_dtypes


def mxq(x, axis, fmt="e4m3"):
    dtype, down = {"e4m3": (ml_dtypes.float8_e4m3fn, 7), "e5m2": (ml_dtypes.float8_e5m2, 14)}[fmt]
    v = np.moveaxis(np.asarray(x, np.float32).astype(ml_dtypes.bfloat16).astype(np.float64), axis, -1)
    blocks = v.reshape(v.shape[:-1] + (-1, 32))
    amax = np.abs(blocks).max(-1, keepdims=True)
    byte = np.maximum(np.where(amax > 0, np.frexp(amax)[1] - 1 + 127, 0) - down, 1)
    scale = np.exp2(byte - 127.0)
    codes = (blocks / scale).astype(np.float32).astype(dtype).astype(np.float64)
    return np.moveaxis((codes * scale).reshape(v.shape), -1, axis)


WIDE = False


def mx_kscale(k):
    if not WIDE:
        return np.ones(k)
    levels = np.array([24, -24, 12, -12, 0])
    if k % 512:
        return np.exp2(np.random.permutation(np.resize(levels, k // 32))).repeat(32)
    a = np.empty((k // 512, 16))
    for p in range(k // 512):
        a[p, :8] = np.random.permutation(np.resize(levels, 8))
        for g in range(8):
            far = levels[np.abs(levels - a[p, g]) >= 10]
            a[p, g + 8] = far[np.random.randint(len(far))]
    return np.exp2(a.ravel()).repeat(32)


def f64(x):
    return np.asarray(x).astype(np.float64)


def striped(idx):
    return np.tile(idx.reshape(-1, 16).T, (8, 1)).astype(np.uint16)


def unstriped(offs):
    return offs[:16].T.reshape(-1).astype(np.int64)


E2M1 = np.array([0.0, 0.5, 1.0, 1.5, 2.0, 3.0, 4.0, 6.0, -0.0, -0.5, -1.0, -1.5, -2.0, -3.0, -4.0, -6.0])


def pack_weight(w, fmt):
    k, n = w.shape
    w = f64(np.asarray(w, np.float32).astype(ml_dtypes.bfloat16)).reshape(k // 32, 32, n)
    amax = np.abs(w).max(1)
    if fmt == "e4m3":
        byte = np.frexp(amax)[1] - 1 + 127 - 7
    else:
        mant, ex = np.frexp(amax / 6.0)
        byte = np.where(mant > 0.5, ex, ex - 1) + 127
    byte = np.clip(np.where(amax > 0, byte, 1), 1, 254)
    scaled = (w * np.exp2(127.0 - byte)[:, None, :]).reshape(k, n).astype(np.float32)
    by_word = np.ascontiguousarray(scaled.reshape(k // 512, 128, 4, n).transpose(0, 1, 3, 2))
    if fmt == "e4m3":
        words = by_word.astype(ml_dtypes.float8_e4m3fn).view(np.uint8)
    else:
        c = by_word.astype(ml_dtypes.float4_e2m1fn).view(np.uint8) & 0xF
        words = (c[..., 0::2] | (c[..., 1::2] << 4)).reshape(k // 512, 128, 2 * n)
    return np.ascontiguousarray(words), np.ascontiguousarray(byte.astype(np.uint8).reshape(k // 512, 16, n))


def unpack_weight(words, scales, fmt):
    g, _, n = scales.shape
    words = np.ascontiguousarray(words).reshape(g, 128, n, -1)
    if fmt == "e4m3":
        vals = words.view(ml_dtypes.float8_e4m3fn).astype(np.float64)
    else:
        nib = np.empty((g, 128, n, 4), np.uint8)
        nib[..., 0::2] = words & 0xF
        nib[..., 1::2] = words >> 4
        vals = E2M1[nib]
    vals = vals * np.repeat(np.exp2(scales.astype(np.float64) - 127.0), 8, axis=1)[..., None]
    return vals.transpose(0, 1, 3, 2).reshape(g * 512, n)


def split(x):
    m, e = np.frexp(f64(x))
    hi = np.ldexp(np.trunc(16.0 * m) / 16.0, e)
    return hi, f64(x) - hi


def sigm(f):
    return 1.0 / (1.0 + np.exp(-np.maximum(f, -700.0)))


K, N, T, J = 1536, 512, 4096, 1024


def setup_inputs():
    n = np.random.standard_normal
    s = mx_kscale(K)[:, None]
    p_tab = pack_weight(n((K, T)) * s, "e4m3")
    return {
        "tab_words": p_tab[0],
        "tab_scales": p_tab[1],
        "wk": (n((K, N)) / np.sqrt(K) / s).astype(np.float32),
        "wv": (n((K, N)) / np.sqrt(K) / s).astype(np.float32),
        "st": (n((N, J))).astype(np.float32),
        "res": (n((N, J))).astype(np.float32),
        "offs": striped(np.random.permutation(T)[:J]),
    }


def reference(tab_words, tab_scales, wk, wv, st, res, offs):
    idx = unstriped(offs)
    tab_ = unpack_weight(tab_words, tab_scales, "e4m3")[:, idx]
    wk_ = mxq(f64(wk), 0, "e4m3")
    wv_hi, wv_lo = split(wv)
    wv_hi_, wv_lo_ = mxq(wv_hi, 0, "e4m3"), mxq(wv_lo, 0, "e4m3")
    ke = wk_.T @ tab_
    ve = wv_hi_.T @ tab_ + wv_lo_.T @ tab_
    gate = sigm(ke * f64(st))
    return f64(res) + gate * ve

@@ -1,0 +1,194 @@
+from contextlib import ExitStack
+
+import concourse.mybir as mybir
+
+K, N, T, J = 1536, 512, 4096, 1024
+FLOPS = 2 * 3 * K * N * J
+
+F32 = mybir.dt.float32
+BF16 = mybir.dt.bfloat16
+I32 = mybir.dt.int32
+U32 = mybir.dt.uint32
+U16 = mybir.dt.uint16
+U8 = mybir.dt.uint8
+FP8X4 = mybir.dt.float8_e4m3fn_x4
+ALU = mybir.AluOpType
+ACT = mybir.ActivationFunctionType
+
+P = 128
+PACK = 4
+K_PASS = P * PACK
+PASSES = K // K_PASS
+HALF = N // 2
+J_TILE = 512
+HI_MASK = 0xFFF0FFF0 - (1 << 32)
+
+
+def tile_list_engram_hl_sig_kernel(tc, tab_words, tab_scales, wk, wv, st, res, offs, out):
+    nc = tc.nc
+    with ExitStack() as ctx:
+        keep = ctx.enter_context(tc.tile_pool(name="keep", bufs=1))
+        work = ctx.enter_context(tc.tile_pool(name="work", bufs=3))
+        psum = ctx.enter_context(tc.psum_pool(name="psum", bufs=4))
+
+        offsets = keep.tile([P, J // 16], U16, name="offsets")
+        planes = keep.tile([P, T // 4], I32, name="planes", align_bytes=64)
+        nc.vector.memset(planes[:], 0)
+        scale_rows = tab_scales.bitcast(I32)
+
+        def load_weight(w, a, cols, name):
+            raw = keep.tile([P, PACK, cols.stop - cols.start], F32, name=name, align_bytes=64)
+            rows = w[a * K_PASS : (a + 1) * K_PASS, cols]
+            nc.sync.dma_start(out=raw[:], in_=rows.rearrange("(p j) n -> p j n", j=PACK))
+            return raw
+
+        def load_table(a):
+            words = keep.tile([P, T], I32, name="table%d" % a, align_bytes=64)
+            nc.sync.dma_start(out=words[:], in_=tab_words[a].rearrange("p t i -> p (t i)").bitcast(I32))
+            return words
+
+        def load_rows(x, nt, name):
+            rows = keep.tile([P, J], F32, name=name, align_bytes=64)
+            nc.sync.dma_start(out=rows[:], in_=x[nt * P : (nt + 1) * P, :])
+            return rows
+
+        halves = [slice(0, HALF), slice(HALF, N)]
+        wv_raw, wk_raw, table, st_sb, res_sb = {}, {}, {}, {}, {}
+
+        def load_wv(a):
+            raw = load_weight(wv, a, slice(0, N), "wv%d" % a)
+            for h in range(2):
+                wv_raw[a, h] = raw[:, :, halves[h]]
+
+        wv_raw[0, 0] = load_weight(wv, 0, halves[0], "wv0a")[:]
+        wv_raw[0, 1] = load_weight(wv, 0, halves[1], "wv0b")[:]
+        nc.sync.dma_start(offsets[:], offs)
+        load_wv(1)
+        for q in range(4):
+            nc.sync.dma_start(out=planes[32 * q : 32 * q + 4 * PASSES, :], in_=scale_rows[:, 4 * q : 4 * q + 4, :])
+        table[0] = load_table(0)
+        wk_raw[0, 0] = load_weight(wk, 0, halves[0], "wk0a")[:]
+        load_wv(2)
+        table[1] = load_table(1)
+        wk_raw[1, 0] = load_weight(wk, 1, halves[0], "wk1a")[:]
+        wk_raw[2, 0] = load_weight(wk, 2, halves[0], "wk2a")[:]
+        table[2] = load_table(2)
+        st_sb[0] = load_rows(st, 0, "st0")
+        wk_raw[0, 1] = load_weight(wk, 0, halves[1], "wk0b")[:]
+        st_sb[1] = load_rows(st, 1, "st1")
+        wk_raw[1, 1] = load_weight(wk, 1, halves[1], "wk1b")[:]
+        wk_raw[2, 1] = load_weight(wk, 2, halves[1], "wk2b")[:]
+        res_sb[0] = load_rows(res, 0, "res0")
+        res_sb[1] = load_rows(res, 1, "res1")
+        st_sb[2] = load_rows(st, 2, "st2")
+        res_sb[2] = load_rows(res, 2, "res2")
+        st_sb[3] = load_rows(st, 3, "st3")
+        res_sb[3] = load_rows(res, 3, "res3")
+
+        def by_rows(raw):
+            return raw.rearrange("p t (c i) -> p c t i", i=4)
+
+        def by_words(grouped):
+            return grouped.rearrange("p (c i t) -> p c t i", i=4, t=PACK)
+
+        def quantize(grouped, name):
+            width = grouped.shape[1] // PACK
+            codes = keep.tile([P, width], U32, name=name + "_codes", align_bytes=64)
+            scales = keep.tile([P, width], U8, name=name + "_scales", align_bytes=64)
+            nc.vector.quantize_mx(out=codes[:].bitcast(FP8X4), scales=scales[:], in_=grouped)
+            return codes[:], scales[:]
+
+        k_mx, hi_mx, lo_mx = {}, {}, {}
+
+        def prepare_wk(a, h):
+            grouped = work.tile([P, HALF * PACK], BF16, name="wk_grouped", align_bytes=64)
+            nc.scalar.copy(out=by_words(grouped[:]), in_=by_rows(wk_raw[a, h]))
+            k_mx[a, h] = quantize(grouped[:], "k%d%d" % (a, h))
+
+        def prepare_wv(a, h):
+            raw = wv_raw[a, h]
+            upper = work.tile([P, HALF * PACK], BF16, name="wv_upper", align_bytes=64)
+            pairs = raw.bitcast(BF16).rearrange("p t (n e) -> p t n e", e=2)
+            nc.scalar.copy(out=by_words(upper[:]), in_=by_rows(pairs[:, :, :, 1]))
+            parts = work.tile([P, 2 * HALF * PACK], BF16, name="wv_parts", align_bytes=64)
+            hi = parts[:, 0 : HALF * PACK]
+            lo = parts[:, HALF * PACK : 2 * HALF * PACK]
+            nc.vector.tensor_scalar(hi.bitcast(I32), upper[:].bitcast(I32), HI_MASK, None, ALU.bitwise_and)
+            nc.vector.tensor_tensor(by_words(lo), by_rows(raw), by_words(hi), ALU.subtract)
+            codes, scales = quantize(parts[:], "v%d%d" % (a, h))
+            hi_mx[a, h] = codes[:, 0:HALF], scales[:, 0:HALF]
+            lo_mx[a, h] = codes[:, HALF : 2 * HALF], scales[:, HALF : 2 * HALF]
+
+        picked_scales = keep.tile([P, J], U8, name="picked_scales", align_bytes=64)
+        picked = [keep.tile([P, J], U32, name="picked%d" % a, align_bytes=64) for a in range(PASSES)]
+
+        def gather_words(a, j0, j1):
+            window = table[a][:].bitcast(U32).indirect(offsets[:, j0 // 16 : j1 // 16])
+            nc.vector.tensor_copy(picked[a][:, j0:j1], window)
+
+        def multiply(acc, weight, nt, jt, a, start, stop):
+            codes, scales = weight[a, nt // 2]
+            n_cols = slice((nt % 2) * P, (nt % 2 + 1) * P)
+            j_cols = slice(jt * J_TILE, (jt + 1) * J_TILE)
+            nc.tensor.matmul_mx(
+                out=acc[:],
+                lhsT=codes[:, n_cols].bitcast(FP8X4),
+                lhsT_scale=scales[:, n_cols],
+                rhs=picked[a][:, j_cols].bitcast(FP8X4),
+                rhs_scale=picked_scales[4 * a : P, j_cols],
+                start=start,
+                stop=stop,
+            )
+
+        def key_pass(ke, nt, jt, a):
+            multiply(ke, k_mx, nt, jt, a, a == 0, a == PASSES - 1)
+
+        def value_pass(ve, nt, jt, a):
+            multiply(ve, hi_mx, nt, jt, a, a == 0, False)
+            multiply(ve, lo_mx, nt, jt, a, False, a == PASSES - 1)
+
+        def finish(ke, ve, nt, jt):
+            j_cols = slice(jt * J_TILE, (jt + 1) * J_TILE)
+            logit = work.tile([P, J_TILE], F32, name="logit")
+            nc.vector.tensor_tensor(logit[:], ke[:], st_sb[nt][:, j_cols], ALU.mult)
+            gate = work.tile([P, J_TILE], F32, name="gate")
+            nc.scalar.activation(gate[:], logit[:], ACT.Sigmoid)
+            gated = work.tile([P, J_TILE], F32, name="gated")
+            nc.vector.tensor_tensor(gated[:], ve[:], gate[:], ALU.mult)
+            result = keep.tile([P, J_TILE], F32, name="result%d%d" % (nt, jt))
+            nc.vector.tensor_tensor(result[:], gated[:], res_sb[nt][:, j_cols], ALU.add)
+            nc.sync.dma_start(out=out[nt * P : (nt + 1) * P, j_cols], in_=result[:])
+
+        first = [(nt, jt) for nt in (0, 1) for jt in (0, 1)]
+        second = [(nt, jt) for nt in (2, 3) for jt in (0, 1)]
+        ke = {u: psum.tile([P, J_TILE], F32, name="ke") for u in first}
+        ve = {u: psum.tile([P, J_TILE], F32, name="ve") for u in first}
+
+        prepare_wv(0, 0)
+        nc.vector.tensor_copy(picked_scales[:], planes[:].bitcast(U8).indirect(offsets[:]))
+        for a in range(PASSES):
+            if a < PASSES - 1:
+                gather_words(a, 0, J)
+            else:
+                gather_words(a, 0, J_TILE)
+                gather_words(a, J_TILE, J)
+            prepare_wk(a, 0)
+            for nt, jt in first:
+                key_pass(ke[nt, jt], nt, jt, a)
+                value_pass(ve[nt, jt], nt, jt, a)
+            if a < PASSES - 1:
+                prepare_wv(a + 1, 0)
+        for a in range(PASSES):
+            prepare_wv(a, 1)
+        for a in range(PASSES):
+            prepare_wk(a, 1)
+        for nt, jt in first:
+            finish(ke[nt, jt], ve[nt, jt], nt, jt)
+        for nt, jt in second:
+            ke2 = psum.tile([P, J_TILE], F32, name="ke")
+            ve2 = psum.tile([P, J_TILE], F32, name="ve")
+            for a in range(PASSES):
+                key_pass(ke2, nt, jt, a)
+            for a in range(PASSES):
+                value_pass(ve2, nt, jt, a)
+            finish(ke2, ve2, nt, jt)

@@ -29,12 +29,14 @@ def tile_list_engram_hl_sig_kernel(tc, tab_words, tab_scales, wk, wv, st, res, o
     with ExitStack() as ctx:
         keep = ctx.enter_context(tc.tile_pool(name="keep", bufs=1))
         work = ctx.enter_context(tc.tile_pool(name="work", bufs=3))
-        psum = ctx.enter_context(tc.psum_pool(name="psum", bufs=4))
+        psum = ctx.enter_context(tc.psum_pool(name="psum", bufs=1))
 
         offsets = keep.tile([P, J // 16], U16, name="offsets")
         planes = keep.tile([P, T // 4], I32, name="planes", align_bytes=64)
         nc.vector.memset(planes[:], 0)
         scale_rows = tab_scales.bitcast(I32)
+        for q in range(4):
+            nc.gpsimd.dma_start(out=planes[32 * q : 32 * q + 4 * PASSES, :], in_=scale_rows[:, 4 * q : 4 * q + 4, :])
 
         def load_weight(w, a, cols, name):
             raw = keep.tile([P, PACK, cols.stop - cols.start], F32, name=name, align_bytes=64)
@@ -55,32 +57,26 @@ def tile_list_engram_hl_sig_kernel(tc, tab_words, tab_scales, wk, wv, st, res, o
         halves = [slice(0, HALF), slice(HALF, N)]
         wv_raw, wk_raw, table, st_sb, res_sb = {}, {}, {}, {}, {}
 
-        def load_wv(a):
-            raw = load_weight(wv, a, slice(0, N), "wv%d" % a)
+        def load_whole(w, raws, a, name):
+            raw = load_weight(w, a, slice(0, N), name)
             for h in range(2):
-                wv_raw[a, h] = raw[:, :, halves[h]]
+                raws[a, h] = raw[:, :, halves[h]]
 
-        wv_raw[0, 0] = load_weight(wv, 0, halves[0], "wv0a")[:]
-        wv_raw[0, 1] = load_weight(wv, 0, halves[1], "wv0b")[:]
+        load_whole(wv, wv_raw, 0, "wv0")
         nc.sync.dma_start(offsets[:], offs)
-        load_wv(1)
-        for q in range(4):
-            nc.sync.dma_start(out=planes[32 * q : 32 * q + 4 * PASSES, :], in_=scale_rows[:, 4 * q : 4 * q + 4, :])
+        load_whole(wv, wv_raw, 1, "wv1")
         table[0] = load_table(0)
-        wk_raw[0, 0] = load_weight(wk, 0, halves[0], "wk0a")[:]
-        load_wv(2)
+        load_whole(wk, wk_raw, 0, "wk0")
         table[1] = load_table(1)
-        wk_raw[1, 0] = load_weight(wk, 1, halves[0], "wk1a")[:]
-        wk_raw[2, 0] = load_weight(wk, 2, halves[0], "wk2a")[:]
+        load_whole(wv, wv_raw, 2, "wv2")
+        load_whole(wk, wk_raw, 1, "wk1")
         table[2] = load_table(2)
+        load_whole(wk, wk_raw, 2, "wk2")
         st_sb[0] = load_rows(st, 0, "st0")
-        wk_raw[0, 1] = load_weight(wk, 0, halves[1], "wk0b")[:]
         st_sb[1] = load_rows(st, 1, "st1")
-        wk_raw[1, 1] = load_weight(wk, 1, halves[1], "wk1b")[:]
-        wk_raw[2, 1] = load_weight(wk, 2, halves[1], "wk2b")[:]
         res_sb[0] = load_rows(res, 0, "res0")
-        res_sb[1] = load_rows(res, 1, "res1")
         st_sb[2] = load_rows(st, 2, "st2")
+        res_sb[1] = load_rows(res, 1, "res1")
         res_sb[2] = load_rows(res, 2, "res2")
         st_sb[3] = load_rows(st, 3, "st3")
         res_sb[3] = load_rows(res, 3, "res3")
@@ -126,10 +122,9 @@ def tile_list_engram_hl_sig_kernel(tc, tab_words, tab_scales, wk, wv, st, res, o
             window = table[a][:].bitcast(U32).indirect(offsets[:, j0 // 16 : j1 // 16])
             nc.vector.tensor_copy(picked[a][:, j0:j1], window)
 
-        def multiply(acc, weight, nt, jt, a, start, stop):
+        def multiply(acc, weight, nt, j_cols, a, start, stop):
             codes, scales = weight[a, nt // 2]
             n_cols = slice((nt % 2) * P, (nt % 2 + 1) * P)
-            j_cols = slice(jt * J_TILE, (jt + 1) * J_TILE)
             nc.tensor.matmul_mx(
                 out=acc[:],
                 lhsT=codes[:, n_cols].bitcast(FP8X4),
@@ -140,55 +135,103 @@ def tile_list_engram_hl_sig_kernel(tc, tab_words, tab_scales, wk, wv, st, res, o
                 stop=stop,
             )
 
-        def key_pass(ke, nt, jt, a):
-            multiply(ke, k_mx, nt, jt, a, a == 0, a == PASSES - 1)
+        def key_pass(ke, nt, j_cols, a):
+            multiply(ke, k_mx, nt, j_cols, a, a == 0, a == PASSES - 1)
 
-        def value_pass(ve, nt, jt, a):
-            multiply(ve, hi_mx, nt, jt, a, a == 0, False)
-            multiply(ve, lo_mx, nt, jt, a, False, a == PASSES - 1)
+        def value_pass(ve, nt, j_cols, a):
+            multiply(ve, hi_mx, nt, j_cols, a, a == 0, False)
+            multiply(ve, lo_mx, nt, j_cols, a, False, a == PASSES - 1)
 
-        def finish(ke, ve, nt, jt):
-            j_cols = slice(jt * J_TILE, (jt + 1) * J_TILE)
+        def make_gate(ke, nt, j_cols):
             logit = work.tile([P, J_TILE], F32, name="logit")
             nc.vector.tensor_tensor(logit[:], ke[:], st_sb[nt][:, j_cols], ALU.mult)
-            gate = work.tile([P, J_TILE], F32, name="gate")
+            gate = work.tile([P, J_TILE], F32, name="gate", bufs=4)
             nc.scalar.activation(gate[:], logit[:], ACT.Sigmoid)
-            gated = work.tile([P, J_TILE], F32, name="gated")
-            nc.vector.tensor_tensor(gated[:], ve[:], gate[:], ALU.mult)
-            result = keep.tile([P, J_TILE], F32, name="result%d%d" % (nt, jt))
-            nc.vector.tensor_tensor(result[:], gated[:], res_sb[nt][:, j_cols], ALU.add)
+            return gate
+
+        def finish(ve, gate, nt, j_cols, adder):
+            width = j_cols.stop - j_cols.start
+            gated = keep.tile([P, width], F32, name="gated%d_%d" % (nt, j_cols.start))
+            nc.vector.tensor_tensor(gated[:], ve[:], gate, ALU.mult)
+            result = keep.tile([P, width], F32, name="result%d_%d" % (nt, j_cols.start))
+            adder.tensor_tensor(result[:], gated[:], res_sb[nt][:, j_cols], ALU.add)
             nc.sync.dma_start(out=out[nt * P : (nt + 1) * P, j_cols], in_=result[:])
 
-        first = [(nt, jt) for nt in (0, 1) for jt in (0, 1)]
-        second = [(nt, jt) for nt in (2, 3) for jt in (0, 1)]
-        ke = {u: psum.tile([P, J_TILE], F32, name="ke") for u in first}
-        ve = {u: psum.tile([P, J_TILE], F32, name="ve") for u in first}
+        j_tiles = [slice(0, J_TILE), slice(J_TILE, J)]
+        units = [(nt, jt) for nt in range(N // P) for jt in (0, 1)]
+        ke = {u: psum.tile([P, J_TILE], F32, name="ke", bufs=2) for u in units[:2]}
+        ve = {u: psum.tile([P, J_TILE], F32, name="ve", bufs=6) for u in units[:6]}
+
+        def value_sweep(a, h):
+            for jt in (0, 1):
+                for nt in (2 * h, 2 * h + 1):
+                    if (nt, jt) in ve:
+                        value_pass(ve[nt, jt], nt, j_tiles[jt], a)
+
+        def key_sweep(a):
+            for jt in (0, 1):
+                for nt in (0, 1):
+                    if (nt, jt) in ke:
+                        key_pass(ke[nt, jt], nt, j_tiles[jt], a)
 
         prepare_wv(0, 0)
+        prepare_wv(0, 1)
+        prepare_wv(1, 0)
+        prepare_wv(1, 1)
+        gather_words(0, 0, J)
         nc.vector.tensor_copy(picked_scales[:], planes[:].bitcast(U8).indirect(offsets[:]))
-        for a in range(PASSES):
-            if a < PASSES - 1:
-                gather_words(a, 0, J)
+        value_sweep(0, 0)
+        value_sweep(0, 1)
+        prepare_wk(0, 0)
+        prepare_wk(0, 1)
+        key_sweep(0)
+        gather_words(1, 0, J)
+        value_sweep(1, 0)
+        value_sweep(1, 1)
+        prepare_wv(2, 0)
+        prepare_wv(2, 1)
+        prepare_wk(1, 0)
+        prepare_wk(1, 1)
+        key_sweep(1)
+        gather_words(2, 0, J_TILE)
+        gather_words(2, J_TILE, J)
+        value_sweep(2, 0)
+        value_sweep(2, 1)
+        prepare_wk(2, 0)
+        prepare_wk(2, 1)
+        key_sweep(2)
+
+        def key_sum(nt, jt):
+            if units.index((nt, jt)) in (4, 5, 6, 7):
+                key = psum.tile([P, J_TILE], F32, name="ve", bufs=6)
             else:
-                gather_words(a, 0, J_TILE)
-                gather_words(a, J_TILE, J)
-            prepare_wk(a, 0)
-            for nt, jt in first:
-                key_pass(ke[nt, jt], nt, jt, a)
-                value_pass(ve[nt, jt], nt, jt, a)
-            if a < PASSES - 1:
-                prepare_wv(a + 1, 0)
-        for a in range(PASSES):
-            prepare_wv(a, 1)
-        for a in range(PASSES):
-            prepare_wk(a, 1)
-        for nt, jt in first:
-            finish(ke[nt, jt], ve[nt, jt], nt, jt)
-        for nt, jt in second:
-            ke2 = psum.tile([P, J_TILE], F32, name="ke")
-            ve2 = psum.tile([P, J_TILE], F32, name="ve")
+                key = psum.tile([P, J_TILE], F32, name="ke", bufs=2)
             for a in range(PASSES):
-                key_pass(ke2, nt, jt, a)
+                key_pass(key, nt, j_tiles[jt], a)
+            return key
+
+        def value_sum(nt, j_cols):
+            value = psum.tile([P, j_cols.stop - j_cols.start], F32, name="ve", bufs=6)
             for a in range(PASSES):
-                value_pass(ve2, nt, jt, a)
-            finish(ke2, ve2, nt, jt)
+                value_pass(value, nt, j_cols, a)
+            return value
+
+        gates = {}
+
+        def gate_of(i):
+            nt, jt = units[i]
+            gates[i] = make_gate(ke[nt, jt] if (nt, jt) in ke else key_sum(nt, jt), nt, j_tiles[jt])
+
+        for i in range(1):
+            gate_of(i)
+        for i, (nt, jt) in enumerate(units):
+            if i + 1 < len(units):
+                gate_of(i + 1)
+            adder = nc.gpsimd if i in (0, 1, 2, 3, 4, 5) else nc.vector
+            if i < len(units) - 1:
+                value = ve[nt, jt] if (nt, jt) in ve else value_sum(nt, j_tiles[jt])
+                finish(value, gates[i][:], nt, j_tiles[jt], adder)
+            else:
+                for j0 in (0, J_TILE // 2):
+                    piece = slice(J_TILE + j0, J_TILE + j0 + J_TILE // 2)
+                    finish(value_sum(nt, piece), gates[i][:, j0 : j0 + J_TILE // 2], nt, piece, adder)

@@ -59,6 +59,7 @@ def tile_list_engram_hl_sig_kernel(tc, tab_words, tab_scales, wk, wv, st, res, o
 
         def load_whole(w, raws, a, name):
             raw = load_weight(w, a, slice(0, N), name)
+            raws[a] = raw[:]
             for h in range(2):
                 raws[a, h] = raw[:, :, halves[h]]
 
@@ -66,11 +67,11 @@ def tile_list_engram_hl_sig_kernel(tc, tab_words, tab_scales, wk, wv, st, res, o
         nc.sync.dma_start(offsets[:], offs)
         load_whole(wv, wv_raw, 1, "wv1")
         table[0] = load_table(0)
-        load_whole(wk, wk_raw, 0, "wk0")
         table[1] = load_table(1)
         load_whole(wv, wv_raw, 2, "wv2")
-        load_whole(wk, wk_raw, 1, "wk1")
+        load_whole(wk, wk_raw, 0, "wk0")
         table[2] = load_table(2)
+        load_whole(wk, wk_raw, 1, "wk1")
         load_whole(wk, wk_raw, 2, "wk2")
         st_sb[0] = load_rows(st, 0, "st0")
         st_sb[1] = load_rows(st, 1, "st1")
@@ -82,10 +83,10 @@ def tile_list_engram_hl_sig_kernel(tc, tab_words, tab_scales, wk, wv, st, res, o
         res_sb[3] = load_rows(res, 3, "res3")
 
         def by_rows(raw):
-            return raw.rearrange("p t (c i) -> p c t i", i=4)
+            return raw.rearrange("p t (c i) -> p c t i", i=2)
 
         def by_words(grouped):
-            return grouped.rearrange("p (c i t) -> p c t i", i=4, t=PACK)
+            return grouped.rearrange("p (c i t) -> p c t i", i=2, t=PACK)
 
         def quantize(grouped, name):
             width = grouped.shape[1] // PACK
@@ -97,23 +98,60 @@ def tile_list_engram_hl_sig_kernel(tc, tab_words, tab_scales, wk, wv, st, res, o
         k_mx, hi_mx, lo_mx = {}, {}, {}
 
         def prepare_wk(a, h):
-            grouped = work.tile([P, HALF * PACK], BF16, name="wk_grouped", align_bytes=64)
-            nc.scalar.copy(out=by_words(grouped[:]), in_=by_rows(wk_raw[a, h]))
-            k_mx[a, h] = quantize(grouped[:], "k%d%d" % (a, h))
+            if (a, h) == (PASSES - 1, 0):
+                codes = keep.tile([P, HALF], U32, name="k_last_codes", align_bytes=64)
+                scales = keep.tile([P, HALF], U8, name="k_last_scales", align_bytes=64)
+                for nt, copy in ((0, nc.vector.tensor_copy), (1, nc.scalar.copy)):
+                    cols = slice(nt * P, (nt + 1) * P)
+                    grouped = keep.tile([P, P * PACK], BF16, name="wk_last%d" % nt, align_bytes=64)
+                    copy(by_words(grouped[:]), by_rows(wk_raw[a, h][:, :, cols]))
+                    nc.vector.quantize_mx(out=codes[:, cols].bitcast(FP8X4), scales=scales[:, cols], in_=grouped[:])
+                k_mx[a, h] = codes[:], scales[:]
+            else:
+                grouped = work.tile([P, HALF * PACK], BF16, name="wk_grouped", bufs=5, align_bytes=64)
+                nc.scalar.copy(out=by_words(grouped[:]), in_=by_rows(wk_raw[a, h]))
+                k_mx[a, h] = quantize(grouped[:], "k%d%d" % (a, h))
 
         def prepare_wv(a, h):
-            raw = wv_raw[a, h]
             upper = work.tile([P, HALF * PACK], BF16, name="wv_upper", align_bytes=64)
-            pairs = raw.bitcast(BF16).rearrange("p t (n e) -> p t n e", e=2)
-            nc.scalar.copy(out=by_words(upper[:]), in_=by_rows(pairs[:, :, :, 1]))
             parts = work.tile([P, 2 * HALF * PACK], BF16, name="wv_parts", align_bytes=64)
-            hi = parts[:, 0 : HALF * PACK]
-            lo = parts[:, HALF * PACK : 2 * HALF * PACK]
-            nc.vector.tensor_scalar(hi.bitcast(I32), upper[:].bitcast(I32), HI_MASK, None, ALU.bitwise_and)
-            nc.vector.tensor_tensor(by_words(lo), by_rows(raw), by_words(hi), ALU.subtract)
+            width = HALF // 2 if (a, h) == (0, 0) else HALF
+            for c0 in range(0, HALF, width):
+                raw = wv_raw[a, h][:, :, c0 : c0 + width]
+                cols = slice(c0 * PACK, (c0 + width) * PACK)
+                pairs = raw.bitcast(BF16).rearrange("p t (n e) -> p t n e", e=2)
+                nc.scalar.copy(out=by_words(upper[:, cols]), in_=by_rows(pairs[:, :, :, 1]))
+                hi = parts[:, cols]
+                lo = parts[:, HALF * PACK + cols.start : HALF * PACK + cols.stop]
+                nc.vector.tensor_scalar(hi.bitcast(I32), upper[:, cols].bitcast(I32), HI_MASK, None, ALU.bitwise_and)
+                nc.vector.tensor_tensor(by_words(lo), by_rows(raw), by_words(hi), ALU.subtract)
             codes, scales = quantize(parts[:], "v%d%d" % (a, h))
             hi_mx[a, h] = codes[:, 0:HALF], scales[:, 0:HALF]
             lo_mx[a, h] = codes[:, HALF : 2 * HALF], scales[:, HALF : 2 * HALF]
+
+        def prepare_wk_whole(a):
+            grouped = work.tile([P, N * PACK], BF16, name="wk_grouped_whole", bufs=2, align_bytes=64)
+            for h in range(2):
+                nc.scalar.copy(out=by_words(grouped[:, h * HALF * PACK : (h + 1) * HALF * PACK]), in_=by_rows(wk_raw[a, h]))
+            codes, scales = quantize(grouped[:], "k%d" % a)
+            for h in range(2):
+                k_mx[a, h] = codes[:, halves[h]], scales[:, halves[h]]
+
+        def prepare_wv_whole(a):
+            raw = wv_raw[a]
+            upper = work.tile([P, N * PACK], BF16, name="wv_upper_whole", bufs=2, align_bytes=64)
+            parts = work.tile([P, 2 * N * PACK], BF16, name="wv_parts_whole", bufs=2, align_bytes=64)
+            pairs = raw.bitcast(BF16).rearrange("p t (n e) -> p t n e", e=2)
+            nc.scalar.copy(out=by_words(upper[:]), in_=by_rows(pairs[:, :, :, 1]))
+            hi = parts[:, 0 : N * PACK]
+            lo = parts[:, N * PACK : 2 * N * PACK]
+            nc.vector.tensor_scalar(hi.bitcast(I32), upper[:].bitcast(I32), HI_MASK, None, ALU.bitwise_and)
+            nc.vector.tensor_tensor(by_words(lo), by_rows(raw), by_words(hi), ALU.subtract)
+            codes, scales = quantize(parts[:], "v%d" % a)
+            for h in range(2):
+                hi_mx[a, h] = codes[:, halves[h]], scales[:, halves[h]]
+                lo_cols = slice(N + h * HALF, N + (h + 1) * HALF)
+                lo_mx[a, h] = codes[:, lo_cols], scales[:, lo_cols]
 
         picked_scales = keep.tile([P, J], U8, name="picked_scales", align_bytes=64)
         picked = [keep.tile([P, J], U32, name="picked%d" % a, align_bytes=64) for a in range(PASSES)]
@@ -151,7 +189,7 @@ def tile_list_engram_hl_sig_kernel(tc, tab_words, tab_scales, wk, wv, st, res, o
 
         def finish(ve, gate, nt, j_cols, adder):
             width = j_cols.stop - j_cols.start
-            gated = keep.tile([P, width], F32, name="gated%d_%d" % (nt, j_cols.start))
+            gated = work.tile([P, width], F32, name="gated", bufs=4)
             nc.vector.tensor_tensor(gated[:], ve[:], gate, ALU.mult)
             result = keep.tile([P, width], F32, name="result%d_%d" % (nt, j_cols.start))
             adder.tensor_tensor(result[:], gated[:], res_sb[nt][:, j_cols], ALU.add)
@@ -182,21 +220,21 @@ def tile_list_engram_hl_sig_kernel(tc, tab_words, tab_scales, wk, wv, st, res, o
         nc.vector.tensor_copy(picked_scales[:], planes[:].bitcast(U8).indirect(offsets[:]))
         value_sweep(0, 0)
         value_sweep(0, 1)
-        prepare_wk(0, 0)
-        prepare_wk(0, 1)
-        key_sweep(0)
         gather_words(1, 0, J)
         value_sweep(1, 0)
         value_sweep(1, 1)
         prepare_wv(2, 0)
         prepare_wv(2, 1)
-        prepare_wk(1, 0)
-        prepare_wk(1, 1)
-        key_sweep(1)
+        prepare_wk(0, 0)
+        prepare_wk(0, 1)
+        key_sweep(0)
         gather_words(2, 0, J_TILE)
         gather_words(2, J_TILE, J)
         value_sweep(2, 0)
         value_sweep(2, 1)
+        prepare_wk(1, 0)
+        prepare_wk(1, 1)
+        key_sweep(1)
         prepare_wk(2, 0)
         prepare_wk(2, 1)
         key_sweep(2)

from contextlib import ExitStack

import concourse.mybir as mybir

K, N, T, J = 1536, 512, 4096, 1024
FLOPS = 2 * 3 * K * N * J

F32 = mybir.dt.float32
BF16 = mybir.dt.bfloat16
I32 = mybir.dt.int32
U32 = mybir.dt.uint32
U16 = mybir.dt.uint16
U8 = mybir.dt.uint8
FP8X4 = mybir.dt.float8_e4m3fn_x4
ALU = mybir.AluOpType
ACT = mybir.ActivationFunctionType

P = 128
PACK = 4
K_PASS = P * PACK
PASSES = K // K_PASS
HALF = N // 2
J_TILE = 512
HI_MASK = 0xFFF0FFF0 - (1 << 32)


def tile_list_engram_hl_sig_kernel(tc, tab_words, tab_scales, wk, wv, st, res, offs, out):
    nc = tc.nc
    with ExitStack() as ctx:
        keep = ctx.enter_context(tc.tile_pool(name="keep", bufs=1))
        work = ctx.enter_context(tc.tile_pool(name="work", bufs=3))
        psum = ctx.enter_context(tc.psum_pool(name="psum", bufs=1))

        offsets = keep.tile([P, J // 16], U16, name="offsets")
        planes = keep.tile([P, T // 4], I32, name="planes", align_bytes=64)
        nc.vector.memset(planes[:], 0)
        scale_rows = tab_scales.bitcast(I32)
        for q in range(4):
            nc.gpsimd.dma_start(out=planes[32 * q : 32 * q + 4 * PASSES, :], in_=scale_rows[:, 4 * q : 4 * q + 4, :])

        def load_weight(w, a, cols, name):
            raw = keep.tile([P, PACK, cols.stop - cols.start], F32, name=name, align_bytes=64)
            rows = w[a * K_PASS : (a + 1) * K_PASS, cols]
            nc.sync.dma_start(out=raw[:], in_=rows.rearrange("(p j) n -> p j n", j=PACK))
            return raw

        def load_table(a):
            words = keep.tile([P, T], I32, name="table%d" % a, align_bytes=64)
            nc.sync.dma_start(out=words[:], in_=tab_words[a].rearrange("p t i -> p (t i)").bitcast(I32))
            return words

        def load_rows(x, nt, name):
            rows = keep.tile([P, J], F32, name=name, align_bytes=64)
            nc.sync.dma_start(out=rows[:], in_=x[nt * P : (nt + 1) * P, :])
            return rows

        halves = [slice(0, HALF), slice(HALF, N)]
        wv_raw, wk_raw, table, st_sb, res_sb = {}, {}, {}, {}, {}

        def load_whole(w, raws, a, name):
            raw = load_weight(w, a, slice(0, N), name)
            raws[a] = raw[:]
            for h in range(2):
                raws[a, h] = raw[:, :, halves[h]]

        load_whole(wv, wv_raw, 0, "wv0")
        nc.sync.dma_start(offsets[:], offs)
        load_whole(wv, wv_raw, 1, "wv1")
        table[0] = load_table(0)
        table[1] = load_table(1)
        load_whole(wv, wv_raw, 2, "wv2")
        load_whole(wk, wk_raw, 0, "wk0")
        table[2] = load_table(2)
        load_whole(wk, wk_raw, 1, "wk1")
        load_whole(wk, wk_raw, 2, "wk2")
        st_sb[0] = load_rows(st, 0, "st0")
        st_sb[1] = load_rows(st, 1, "st1")
        res_sb[0] = load_rows(res, 0, "res0")
        st_sb[2] = load_rows(st, 2, "st2")
        res_sb[1] = load_rows(res, 1, "res1")
        res_sb[2] = load_rows(res, 2, "res2")
        st_sb[3] = load_rows(st, 3, "st3")
        res_sb[3] = load_rows(res, 3, "res3")

        def by_rows(raw):
            return raw.rearrange("p t (c i) -> p c t i", i=2)

        def by_words(grouped):
            return grouped.rearrange("p (c i t) -> p c t i", i=2, t=PACK)

        def quantize(grouped, name):
            width = grouped.shape[1] // PACK
            codes = keep.tile([P, width], U32, name=name + "_codes", align_bytes=64)
            scales = keep.tile([P, width], U8, name=name + "_scales", align_bytes=64)
            nc.vector.quantize_mx(out=codes[:].bitcast(FP8X4), scales=scales[:], in_=grouped)
            return codes[:], scales[:]

        k_mx, hi_mx, lo_mx = {}, {}, {}

        def prepare_wk(a, h):
            if (a, h) == (PASSES - 1, 0):
                codes = keep.tile([P, HALF], U32, name="k_last_codes", align_bytes=64)
                scales = keep.tile([P, HALF], U8, name="k_last_scales", align_bytes=64)
                for nt, copy in ((0, nc.vector.tensor_copy), (1, nc.scalar.copy)):
                    cols = slice(nt * P, (nt + 1) * P)
                    grouped = keep.tile([P, P * PACK], BF16, name="wk_last%d" % nt, align_bytes=64)
                    copy(by_words(grouped[:]), by_rows(wk_raw[a, h][:, :, cols]))
                    nc.vector.quantize_mx(out=codes[:, cols].bitcast(FP8X4), scales=scales[:, cols], in_=grouped[:])
                k_mx[a, h] = codes[:], scales[:]
            else:
                grouped = work.tile([P, HALF * PACK], BF16, name="wk_grouped", bufs=5, align_bytes=64)
                nc.scalar.copy(out=by_words(grouped[:]), in_=by_rows(wk_raw[a, h]))
                k_mx[a, h] = quantize(grouped[:], "k%d%d" % (a, h))

        def prepare_wv(a, h):
            upper = work.tile([P, HALF * PACK], BF16, name="wv_upper", align_bytes=64)
            parts = work.tile([P, 2 * HALF * PACK], BF16, name="wv_parts", align_bytes=64)
            width = HALF // 2 if (a, h) == (0, 0) else HALF
            for c0 in range(0, HALF, width):
                raw = wv_raw[a, h][:, :, c0 : c0 + width]
                cols = slice(c0 * PACK, (c0 + width) * PACK)
                pairs = raw.bitcast(BF16).rearrange("p t (n e) -> p t n e", e=2)
                nc.scalar.copy(out=by_words(upper[:, cols]), in_=by_rows(pairs[:, :, :, 1]))
                hi = parts[:, cols]
                lo = parts[:, HALF * PACK + cols.start : HALF * PACK + cols.stop]
                nc.vector.tensor_scalar(hi.bitcast(I32), upper[:, cols].bitcast(I32), HI_MASK, None, ALU.bitwise_and)
                nc.vector.tensor_tensor(by_words(lo), by_rows(raw), by_words(hi), ALU.subtract)
            codes, scales = quantize(parts[:], "v%d%d" % (a, h))
            hi_mx[a, h] = codes[:, 0:HALF], scales[:, 0:HALF]
            lo_mx[a, h] = codes[:, HALF : 2 * HALF], scales[:, HALF : 2 * HALF]

        def prepare_wk_whole(a):
            grouped = work.tile([P, N * PACK], BF16, name="wk_grouped_whole", bufs=2, align_bytes=64)
            for h in range(2):
                nc.scalar.copy(out=by_words(grouped[:, h * HALF * PACK : (h + 1) * HALF * PACK]), in_=by_rows(wk_raw[a, h]))
            codes, scales = quantize(grouped[:], "k%d" % a)
            for h in range(2):
                k_mx[a, h] = codes[:, halves[h]], scales[:, halves[h]]

        def prepare_wv_whole(a):
            raw = wv_raw[a]
            upper = work.tile([P, N * PACK], BF16, name="wv_upper_whole", bufs=2, align_bytes=64)
            parts = work.tile([P, 2 * N * PACK], BF16, name="wv_parts_whole", bufs=2, align_bytes=64)
            pairs = raw.bitcast(BF16).rearrange("p t (n e) -> p t n e", e=2)
            nc.scalar.copy(out=by_words(upper[:]), in_=by_rows(pairs[:, :, :, 1]))
            hi = parts[:, 0 : N * PACK]
            lo = parts[:, N * PACK : 2 * N * PACK]
            nc.vector.tensor_scalar(hi.bitcast(I32), upper[:].bitcast(I32), HI_MASK, None, ALU.bitwise_and)
            nc.vector.tensor_tensor(by_words(lo), by_rows(raw), by_words(hi), ALU.subtract)
            codes, scales = quantize(parts[:], "v%d" % a)
            for h in range(2):
                hi_mx[a, h] = codes[:, halves[h]], scales[:, halves[h]]
                lo_cols = slice(N + h * HALF, N + (h + 1) * HALF)
                lo_mx[a, h] = codes[:, lo_cols], scales[:, lo_cols]

        picked_scales = keep.tile([P, J], U8, name="picked_scales", align_bytes=64)
        picked = [keep.tile([P, J], U32, name="picked%d" % a, align_bytes=64) for a in range(PASSES)]

        def gather_words(a, j0, j1):
            window = table[a][:].bitcast(U32).indirect(offsets[:, j0 // 16 : j1 // 16])
            nc.vector.tensor_copy(picked[a][:, j0:j1], window)

        def multiply(acc, weight, nt, j_cols, a, start, stop):
            codes, scales = weight[a, nt // 2]
            n_cols = slice((nt % 2) * P, (nt % 2 + 1) * P)
            nc.tensor.matmul_mx(
                out=acc[:],
                lhsT=codes[:, n_cols].bitcast(FP8X4),
                lhsT_scale=scales[:, n_cols],
                rhs=picked[a][:, j_cols].bitcast(FP8X4),
                rhs_scale=picked_scales[4 * a : P, j_cols],
                start=start,
                stop=stop,
            )

        def key_pass(ke, nt, j_cols, a):
            multiply(ke, k_mx, nt, j_cols, a, a == 0, a == PASSES - 1)

        def value_pass(ve, nt, j_cols, a):
            multiply(ve, hi_mx, nt, j_cols, a, a == 0, False)
            multiply(ve, lo_mx, nt, j_cols, a, False, a == PASSES - 1)

        def make_gate(ke, nt, j_cols):
            logit = work.tile([P, J_TILE], F32, name="logit")
            nc.vector.tensor_tensor(logit[:], ke[:], st_sb[nt][:, j_cols], ALU.mult)
            gate = work.tile([P, J_TILE], F32, name="gate", bufs=4)
            nc.scalar.activation(gate[:], logit[:], ACT.Sigmoid)
            return gate

        def finish(ve, gate, nt, j_cols, adder):
            width = j_cols.stop - j_cols.start
            gated = work.tile([P, width], F32, name="gated", bufs=4)
            nc.vector.tensor_tensor(gated[:], ve[:], gate, ALU.mult)
            result = keep.tile([P, width], F32, name="result%d_%d" % (nt, j_cols.start))
            adder.tensor_tensor(result[:], gated[:], res_sb[nt][:, j_cols], ALU.add)
            nc.sync.dma_start(out=out[nt * P : (nt + 1) * P, j_cols], in_=result[:])

        j_tiles = [slice(0, J_TILE), slice(J_TILE, J)]
        units = [(nt, jt) for nt in range(N // P) for jt in (0, 1)]
        ke = {u: psum.tile([P, J_TILE], F32, name="ke", bufs=2) for u in units[:2]}
        ve = {u: psum.tile([P, J_TILE], F32, name="ve", bufs=6) for u in units[:6]}

        def value_sweep(a, h):
            for jt in (0, 1):
                for nt in (2 * h, 2 * h + 1):
                    if (nt, jt) in ve:
                        value_pass(ve[nt, jt], nt, j_tiles[jt], a)

        def key_sweep(a):
            for jt in (0, 1):
                for nt in (0, 1):
                    if (nt, jt) in ke:
                        key_pass(ke[nt, jt], nt, j_tiles[jt], a)

        prepare_wv(0, 0)
        prepare_wv(0, 1)
        prepare_wv(1, 0)
        prepare_wv(1, 1)
        gather_words(0, 0, J)
        nc.vector.tensor_copy(picked_scales[:], planes[:].bitcast(U8).indirect(offsets[:]))
        value_sweep(0, 0)
        value_sweep(0, 1)
        gather_words(1, 0, J)
        value_sweep(1, 0)
        value_sweep(1, 1)
        prepare_wv(2, 0)
        prepare_wv(2, 1)
        prepare_wk(0, 0)
        prepare_wk(0, 1)
        key_sweep(0)
        gather_words(2, 0, J_TILE)
        gather_words(2, J_TILE, J)
        value_sweep(2, 0)
        value_sweep(2, 1)
        prepare_wk(1, 0)
        prepare_wk(1, 1)
        key_sweep(1)
        prepare_wk(2, 0)
        prepare_wk(2, 1)
        key_sweep(2)

        def key_sum(nt, jt):
            if units.index((nt, jt)) in (4, 5, 6, 7):
                key = psum.tile([P, J_TILE], F32, name="ve", bufs=6)
            else:
                key = psum.tile([P, J_TILE], F32, name="ke", bufs=2)
            for a in range(PASSES):
                key_pass(key, nt, j_tiles[jt], a)
            return key

        def value_sum(nt, j_cols):
            value = psum.tile([P, j_cols.stop - j_cols.start], F32, name="ve", bufs=6)
            for a in range(PASSES):
                value_pass(value, nt, j_cols, a)
            return value

        gates = {}

        def gate_of(i):
            nt, jt = units[i]
            gates[i] = make_gate(ke[nt, jt] if (nt, jt) in ke else key_sum(nt, jt), nt, j_tiles[jt])

        for i in range(1):
            gate_of(i)
        for i, (nt, jt) in enumerate(units):
            if i + 1 < len(units):
                gate_of(i + 1)
            adder = nc.gpsimd if i in (0, 1, 2, 3, 4, 5) else nc.vector
            if i < len(units) - 1:
                value = ve[nt, jt] if (nt, jt) in ve else value_sum(nt, j_tiles[jt])
                finish(value, gates[i][:], nt, j_tiles[jt], adder)
            else:
                for j0 in (0, J_TILE // 2):
                    piece = slice(J_TILE + j0, J_TILE + j0 + J_TILE // 2)
                    finish(value_sum(nt, piece), gates[i][:, j0 : j0 + J_TILE // 2], nt, piece, adder)
